import numpy as np
import ml_dtypes


def mxq(x, axis, fmt="e4m3"):
    dtype, down = {"e4m3": (ml_dtypes.float8_e4m3fn, 7), "e5m2": (ml_dtypes.float8_e5m2, 14)}[fmt]
    v = np.moveaxis(np.asarray(x, np.float32).astype(ml_dtypes.bfloat16).astype(np.float64), axis, -1)
    blocks = v.reshape(v.shape[:-1] + (-1, 32))
    amax = np.abs(blocks).max(-1, keepdims=True)
    byte = np.maximum(np.where(amax > 0, np.frexp(amax)[1] - 1 + 127, 0) - down, 1)
    scale = np.exp2(byte - 127.0)
    codes = (blocks / scale).astype(np.float32).astype(dtype).astype(np.float64)
    return np.moveaxis((codes * scale).reshape(v.shape), -1, axis)


WIDE = False


def mx_kscale(k):
    if not WIDE:
        return np.ones(k)
    levels = np.array([10, -10, 5, -5, 0])
    if k % 512:
        return np.exp2(np.random.permutation(np.resize(levels, k // 32))).repeat(32)
    a = np.empty((k // 512, 16))
    for p in range(k // 512):
        a[p, :8] = np.random.permutation(np.resize(levels, 8))
        for g in range(8):
            far = levels[np.abs(levels - a[p, g]) >= 10]
            a[p, g + 8] = far[np.random.randint(len(far))]
    return np.exp2(a.ravel()).repeat(32)


BF16 = ml_dtypes.bfloat16


def bf(x):
    return np.asarray(x, np.float32).astype(BF16)


def f64(x):
    return np.asarray(x).astype(np.float64)


E2M1 = np.array([0.0, 0.5, 1.0, 1.5, 2.0, 3.0, 4.0, 6.0, -0.0, -0.5, -1.0, -1.5, -2.0, -3.0, -4.0, -6.0])


def pack_weight(w, fmt):
    k, n = w.shape
    w = f64(bf(w)).reshape(k // 32, 32, n)
    amax = np.abs(w).max(1)
    if fmt == "e4m3":
        byte = np.frexp(amax)[1] - 1 + 127 - 7
    else:
        mant, ex = np.frexp(amax / 6.0)
        byte = np.where(mant > 0.5, ex, ex - 1) + 127
    byte = np.clip(np.where(amax > 0, byte, 1), 1, 254)
    scaled = (w * np.exp2(127.0 - byte)[:, None, :]).reshape(k, n).astype(np.float32)
    by_word = np.ascontiguousarray(scaled.reshape(k // 512, 128, 4, n).transpose(0, 1, 3, 2))
    if fmt == "e4m3":
        words = by_word.astype(ml_dtypes.float8_e4m3fn).view(np.uint8)
    else:
        c = by_word.astype(ml_dtypes.float4_e2m1fn).view(np.uint8) & 0xF
        words = c[..., 0::2] | (c[..., 1::2] << 4)
    return np.ascontiguousarray(words), np.ascontiguousarray(byte.astype(np.uint8).reshape(k // 512, 16, n))


def unpack_weight(words, scales, fmt):
    g, p, n, _ = words.shape
    if fmt == "e4m3":
        vals = np.ascontiguousarray(words).view(ml_dtypes.float8_e4m3fn).astype(np.float64)
    else:
        nib = np.empty((g, p, n, 4), np.uint8)
        nib[..., 0::2] = words & 0xF
        nib[..., 1::2] = words >> 4
        vals = E2M1[nib]
    vals = vals * np.repeat(np.exp2(scales.astype(np.float64) - 127.0), 8, axis=1)[..., None]
    return vals.transpose(0, 1, 3, 2).reshape(g * 512, n)
def pack4(w):
    words, scales = pack_weight(w, "e2m1")
    return words.reshape(words.shape[0], 128, -1), scales


def unpack4(words, scales):
    return unpack_weight(words.reshape(words.shape[0], 128, -1, 2), scales, "e2m1")


def planes(Y):
    n, m = Y.shape
    b = f64(bf(Y)).reshape(n // 32, 32, m)
    amax = np.abs(b).max(1)
    byte = np.clip(np.where(amax > 0, np.frexp(amax)[1] - 1 + 127 - 7, 1), 1, 254)
    codes = (b * np.exp2(127.0 - byte)[:, None, :]).reshape(n, m).astype(np.float32).astype(ml_dtypes.float8_e4m3fn).view(np.uint8)
    words = codes.reshape(n // 512, 128, 4, m).transpose(0, 1, 3, 2)
    return np.ascontiguousarray(words), np.ascontiguousarray(byte.astype(np.uint8).reshape(n // 512, 16, m))


E, C, D, F = 4, 512, 1024, 1536
BIAS_MEAN = 1.2
BIAS_NOISE = 0.3
SPREAD = 0.4


def setup_inputs():
    s = mx_kscale(D)
    X = np.random.standard_normal((D, E * C)) * s[:, None]
    x_words, x_scales = pack_weight(X, "e4m3")
    size = np.exp(SPREAD * np.random.standard_normal((E, F)))
    w_up = np.random.standard_normal((E, D, F)) / np.sqrt(D)
    w_up = w_up * size[:, None, :] / s[None, :, None]
    b_up = size * (BIAS_MEAN + BIAS_NOISE * np.random.standard_normal((E, F)))
    router_weight = 1.0 / (1.0 + np.exp(-np.random.standard_normal((E, C))))
    return {"x_words": x_words, "x_scales": x_scales, "w_up": bf(w_up),
            "b_up": bf(b_up), "router_weight": bf(router_weight)}


def reference(x_words, x_scales, w_up, b_up, router_weight):
    x = unpack_weight(x_words, x_scales, "e4m3").T.reshape(E, C, D)
    w = mxq(f64(w_up), 1, "e4m3")
    a = x @ w
    h = np.maximum(a + f64(b_up)[:, None, :], 0.0)
    y = h * h * f64(router_weight)[:, :, None]
    Y = y.reshape(E * C, F).T
    words, scales = planes(Y)
    return y, words, scales

@@ -1,0 +1,283 @@
+from contextlib import ExitStack
+
+import concourse.mybir as mybir
+from concourse.masks import make_identity
+
+E, C, D, F = 4, 512, 1024, 1536
+FLOPS = 2 * E * C * D * F
+
+F32 = mybir.dt.float32
+BF16 = mybir.dt.bfloat16
+I32 = mybir.dt.int32
+U32 = mybir.dt.uint32
+U8 = mybir.dt.uint8
+FP8X4 = mybir.dt.float8_e4m3fn_x4
+ACT = mybir.ActivationFunctionType
+ALU = mybir.AluOpType
+
+P = 128
+PACK = 4
+K_PASS = P * PACK
+PASSES = D // K_PASS
+GROUPS = F // K_PASS
+CHUNK = 256
+STEPS_PER_EXPERT = F // CHUNK
+STEPS = E * STEPS_PER_EXPERT
+
+
+def scalar_columns(s):
+    if s == 0:
+        return 88
+    if s in (1, 2):
+        return 112
+    if s == 3:
+        return 64
+    return 32
+
+
+def tile_expert_up_squared_relu_g6_kernel(
+    tc, x_words, x_scales, w_up, b_up, router_weight, out_0, out_1, out_2
+):
+    nc = tc.nc
+
+    with ExitStack() as ctx:
+        keep = ctx.enter_context(tc.tile_pool(name="keep", bufs=1))
+        work = ctx.enter_context(tc.tile_pool(name="work", bufs=3))
+        psum = ctx.enter_context(tc.psum_pool(name="psum", bufs=3))
+        ctx.enter_context(tc.manual_schedule())
+
+        x_codes = keep.tile([P, PASSES, E * C], U32, align_bytes=64)
+        x_plane = keep.tile([P, PASSES, E * C], U8, align_bytes=64)
+        y_plane = keep.tile([P, GROUPS, E * C], U8, align_bytes=64)
+        rows = keep.tile([P, P], BF16)
+        columns = keep.tile([P, 64], F32)
+        identity_bf16 = keep.tile([P, P], BF16)
+        identity_f32 = keep.tile([P, P], F32)
+
+        nc.vector.memset(x_plane[:].rearrange("p g n -> p (g n)").bitcast(I32), 0)
+        nc.gpsimd.memset(rows[:], 0.0)
+        nc.gpsimd.dma_start(out=rows[0:48, :], in_=b_up.rearrange("e (j p) -> (e j) p", p=P))
+        nc.gpsimd.dma_start(out=rows[48:64, :], in_=router_weight.rearrange("e (m p) -> (e m) p", p=P))
+        make_identity(nc, identity_bf16[:])
+        make_identity(nc, identity_f32[:])
+
+        w_raw = {}
+
+        def load_w(e, cols):
+            if e not in w_raw:
+                w_raw[e] = work.tile([P, PASSES, PACK, F], BF16, name="w_raw", tag="w_raw")
+            for g in range(PASSES):
+                src = w_up[e, g * K_PASS : (g + 1) * K_PASS, cols].rearrange("(p t) f -> p t f", t=PACK)
+                nc.sync.dma_start(out=w_raw[e][:, g, :, cols], in_=src)
+
+        def load_x_codes(tokens):
+            src = x_words.rearrange("g p n t -> p g (n t)")
+            src = src[:, :, PACK * tokens.start : PACK * tokens.stop].bitcast(I32)
+            nc.sync.dma_start(out=x_codes[:, :, tokens].bitcast(I32), in_=src)
+
+        def load_x_scales(tokens):
+            for q in range(4):
+                src = x_scales[:, 4 * q : 4 * q + 4, tokens].rearrange("g r n -> r g n").bitcast(I32)
+                nc.sync.dma_start(out=x_plane[32 * q : 32 * q + 4, :, tokens].bitcast(I32), in_=src)
+
+        load_w(0, slice(0, 256))
+        load_x_scales(slice(0, C))
+        load_x_codes(slice(0, C))
+        load_w(0, slice(256, 512))
+        load_w(0, slice(512, 1024))
+        load_w(0, slice(1024, F))
+        load_x_scales(slice(C, E * C))
+        load_x_codes(slice(C, E * C))
+        load_w(1, slice(0, F))
+        load_w(2, slice(0, F))
+
+        w_grouped, w_codes, w_plane = {}, {}, {}
+        acc, h, h_t, squares, y, y_bf16, words_t, y_grouped, y_codes = {}, {}, {}, {}, {}, {}, {}, {}, {}
+
+        def interleave_views(s, lo, hi):
+            e, first = divmod(s * CHUNK, F)
+            dst = w_grouped[s][:, :, lo:hi, :]
+            src = w_raw[e][:, :, :, first + lo : first + hi]
+            return dst, src
+
+        def interleave_scalar(s):
+            w_grouped[s] = work.tile([P, PASSES, CHUNK, PACK], BF16, name="w_grouped", tag="w_grouped", align_bytes=64)
+            dst, src = interleave_views(s, 0, scalar_columns(s))
+            if s == 0:
+                nc.scalar.activation(out=dst, in_=src.rearrange("p g t c -> p g c t"), func=ACT.Copy)
+            else:
+                nc.scalar.copy(
+                    out=dst.rearrange("p g (c i) t -> p g c t i", i=4),
+                    in_=src.rearrange("p g t (c i) -> p g c t i", i=4),
+                )
+
+        def interleave_vector(s):
+            dst, src = interleave_views(s, scalar_columns(s), CHUNK)
+            nc.vector.tensor_copy(
+                out=dst.rearrange("p g (c i) t -> p g c t i", i=4),
+                in_=src.rearrange("p g t (c i) -> p g c t i", i=4),
+            )
+
+        def quantize_w(s):
+            w_codes[s] = work.tile([P, PASSES * CHUNK], U32, name="w_codes", tag="w_codes", bufs=4, align_bytes=64)
+            w_plane[s] = work.tile([P, PASSES * CHUNK], U8, name="w_plane", tag="w_plane", bufs=4, align_bytes=64)
+            nc.vector.quantize_mx(
+                out=w_codes[s][:].bitcast(FP8X4),
+                scales=w_plane[s][:],
+                in_=w_grouped[s][:].rearrange("p g c t -> p (g c t)"),
+            )
+
+        def multiply(s):
+            e = s // STEPS_PER_EXPERT
+            tokens = slice(e * C, (e + 1) * C)
+            for j in range(2):
+                acc[s, j] = psum.tile([P, C], F32, name="acc", tag="acc")
+                for g in range(PASSES):
+                    cols = slice(g * CHUNK + j * P, g * CHUNK + (j + 1) * P)
+                    nc.tensor.matmul_mx(
+                        out=acc[s, j][:],
+                        lhsT=w_codes[s][:, cols].bitcast(FP8X4),
+                        lhsT_scale=w_plane[s][:, cols],
+                        rhs=x_codes[:, g, tokens].bitcast(FP8X4),
+                        rhs_scale=x_plane[:, g, tokens],
+                        start=(g == 0),
+                        stop=(g == PASSES - 1),
+                    )
+
+        def bias_relu(s):
+            unit, half = divmod(s, 2)
+            if half == 0:
+                h[unit] = work.tile([P, 4, C], F32, name="h", tag="h", bufs=2)
+            for j in range(2):
+                col = 2 * s + j
+                nc.scalar.activation(
+                    out=h[unit][:, 2 * half + j, :], in_=acc[s, j][:], func=ACT.Relu, bias=columns[:, col : col + 1]
+                )
+
+        def transpose_h(s):
+            unit, half = divmod(s, 2)
+            for i in range(2):
+                m = 2 * half + i
+                h_t[s, i] = psum.tile([P, K_PASS], F32, name="h_t", tag="h_t")
+                for j in range(4):
+                    nc.tensor.transpose(
+                        h_t[s, i][:, j * P : (j + 1) * P], h[unit][:, j, m * P : (m + 1) * P], identity_f32[:]
+                    )
+
+        def square(s):
+            squares[s] = work.tile([P, 2, K_PASS], F32, name="squares", tag="squares")
+            for i in range(2):
+                nc.scalar.activation(out=squares[s][:, i, :], in_=h_t[s, i][:], func=ACT.Square)
+
+        def place(s):
+            unit, half = divmod(s, 2)
+            e, g = divmod(unit, GROUPS)
+            return e, g, half
+
+        def weigh(s):
+            e, g, half = place(s)
+            if g == 0:
+                y[e, half] = work.tile([P, 2, F], F32, name="y", tag="y", bufs=4)
+            for i in range(2):
+                col = 48 + 4 * e + 2 * half + i
+                nc.vector.tensor_scalar(
+                    out=y[e, half][:, i, g * K_PASS : (g + 1) * K_PASS],
+                    in0=squares[s][:, i, :],
+                    scalar1=columns[:, col : col + 1],
+                    scalar2=None,
+                    op0=ALU.mult,
+                )
+
+        def store_y(s):
+            e, g, half = place(s)
+            dst = out_0[e, half * 2 * P : (half + 1) * 2 * P, :].rearrange("(i p) f -> p i f", p=P)
+            if e == E - 1:
+                cols = slice(g * K_PASS, (g + 1) * K_PASS)
+                nc.sync.dma_start(out=dst[:, :, cols], in_=y[e, half][:, :, cols])
+            elif g == GROUPS - 1:
+                nc.sync.dma_start(out=dst, in_=y[e, half][:])
+
+        def round_y(s):
+            e, g, half = place(s)
+            y_bf16[s] = work.tile([P, 2 * K_PASS], BF16, name="y_bf16", tag="y_bf16")
+            nc.vector.tensor_copy(
+                out=y_bf16[s][:].rearrange("p (i u c b) -> p i u c b", i=2, u=2, b=2),
+                in_=y[e, half][:, :, g * K_PASS : (g + 1) * K_PASS].rearrange("p i (c u b) -> p i u c b", u=2, b=2),
+            )
+
+        def transpose_y(s):
+            words_t[s] = psum.tile([P, 4, P], F32, name="words_t", tag="words_t", bufs=2)
+            pairs = y_bf16[s][:].bitcast(F32)
+            for k in range(4):
+                nc.tensor.transpose(words_t[s][:, k, :], pairs[:, k * P : (k + 1) * P], identity_f32[:])
+
+        def group_y(s):
+            y_grouped[s] = work.tile([P, 2 * P * PACK], BF16, name="y_grouped", tag="y_grouped", align_bytes=64)
+            nc.scalar.copy(
+                out=y_grouped[s][:].bitcast(F32).rearrange("p (i n u) -> p i n u", i=2, u=2),
+                in_=words_t[s][:].rearrange("p (i u) n -> p i n u", u=2),
+            )
+
+        def quantize_y(s):
+            e, g, half = place(s)
+            unit = s // 2
+            if half == 0:
+                y_codes[unit] = work.tile([P, C], U32, name="y_codes", tag="y_codes", bufs=6, align_bytes=64)
+            first = e * C + half * 2 * P
+            nc.vector.quantize_mx(
+                out=y_codes[unit][:, half * 2 * P : (half + 1) * 2 * P].bitcast(FP8X4),
+                scales=y_plane[:, g, first : first + 2 * P],
+                in_=y_grouped[s][:],
+            )
+
+        def store_planes(s):
+            e, g, half = place(s)
+            if half == 0:
+                return
+            dst = out_1[g].rearrange("p n t -> p (n t)")[:, PACK * e * C : PACK * (e + 1) * C].bitcast(I32)
+            nc.sync.dma_start(out=dst, in_=y_codes[s // 2][:].bitcast(I32))
+            if e == E - 1:
+                for q in range(4):
+                    nc.sync.dma_start(
+                        out=out_2[g, 4 * q : 4 * q + 4, :].bitcast(I32),
+                        in_=y_plane[32 * q : 32 * q + 4, g, :].bitcast(I32),
+                    )
+
+        def live(s):
+            return 0 <= s < STEPS
+
+        for s in range(-3, STEPS + 5):
+            if s == -2:
+                rows_t = psum.tile([P, P], BF16, name="rows_t", tag="words_t", bufs=2)
+                nc.tensor.transpose(rows_t[:], rows[:], identity_bf16[:])
+                nc.scalar.copy(out=columns[:], in_=rows_t[:, 0:64])
+            if live(s):
+                multiply(s)
+            if live(s - 2):
+                transpose_h(s - 2)
+            if live(s - 4):
+                transpose_y(s - 4)
+            if live(s):
+                bias_relu(s)
+            if live(s - 2):
+                square(s - 2)
+            if live(s - 4):
+                group_y(s - 4)
+            if live(s + 3):
+                interleave_scalar(s + 3)
+            if live(s + 2):
+                interleave_vector(s + 2)
+            if live(s - 3):
+                weigh(s - 3)
+            if live(s + 2):
+                quantize_w(s + 2)
+            if live(s - 3):
+                round_y(s - 3)
+            if live(s - 5):
+                quantize_y(s - 5)
+            if s + 2 == STEPS_PER_EXPERT - 1:
+                load_w(3, slice(0, F))
+            if live(s - 3):
+                store_y(s - 3)
+            if live(s - 5):
+                store_planes(s - 5)

@@ -25,14 +25,11 @@ STEPS_PER_EXPERT = F // CHUNK
 STEPS = E * STEPS_PER_EXPERT
 
 
+W_CUTS = [[0, 512, 1024, F], [0, 512, F], [0, F], [0, F]]
+
+
 def scalar_columns(s):
-    if s == 0:
-        return 88
-    if s in (1, 2):
-        return 112
-    if s == 3:
-        return 64
-    return 32
+    return 128 if s < 4 else 64
 
 
 def tile_expert_up_squared_relu_g6_kernel(
@@ -46,77 +43,84 @@ def tile_expert_up_squared_relu_g6_kernel(
         psum = ctx.enter_context(tc.psum_pool(name="psum", bufs=3))
         ctx.enter_context(tc.manual_schedule())
 
-        x_codes = keep.tile([P, PASSES, E * C], U32, align_bytes=64)
-        x_plane = keep.tile([P, PASSES, E * C], U8, align_bytes=64)
-        y_plane = keep.tile([P, GROUPS, E * C], U8, align_bytes=64)
+        x_codes = [keep.tile([P, PASSES, C], U32, name="x_codes%d" % e, align_bytes=64) for e in range(E)]
+        x_plane_first = keep.tile([P, PASSES, C], U8, align_bytes=64)
+        x_plane_rest = keep.tile([P, PASSES, (E - 1) * C], U8, align_bytes=64)
+        y_plane_rest = keep.tile([P, GROUPS, (E - 1) * C], U8, align_bytes=64)
+        y_plane_last = keep.tile([P, GROUPS, C], U8, align_bytes=64)
         rows = keep.tile([P, P], BF16)
+        rows_f32 = keep.tile([P, P], F32)
         columns = keep.tile([P, 64], F32)
-        identity_bf16 = keep.tile([P, P], BF16)
-        identity_f32 = keep.tile([P, P], F32)
+        identity = keep.tile([P, P], F32)
 
-        nc.vector.memset(x_plane[:].rearrange("p g n -> p (g n)").bitcast(I32), 0)
-        nc.gpsimd.memset(rows[:], 0.0)
-        nc.gpsimd.dma_start(out=rows[0:48, :], in_=b_up.rearrange("e (j p) -> (e j) p", p=P))
-        nc.gpsimd.dma_start(out=rows[48:64, :], in_=router_weight.rearrange("e (m p) -> (e m) p", p=P))
-        make_identity(nc, identity_bf16[:])
-        make_identity(nc, identity_f32[:])
+        nc.vector.memset(rows[:], 0.0)
+        nc.vector.memset(x_plane_first[:].rearrange("p g n -> p (g n)").bitcast(I32), 0)
+        nc.vector.memset(x_plane_rest[:].rearrange("p g n -> p (g n)").bitcast(I32), 0)
+        nc.scalar.dma_start(out=rows[0:48, :], in_=b_up.rearrange("e (j p) -> (e j) p", p=P))
+        nc.scalar.dma_start(out=rows[48:64, :], in_=router_weight.rearrange("e (m p) -> (e m) p", p=P))
+        make_identity(nc, identity[:])
 
         w_raw = {}
 
-        def load_w(e, cols):
-            if e not in w_raw:
-                w_raw[e] = work.tile([P, PASSES, PACK, F], BF16, name="w_raw", tag="w_raw")
+        def w_piece(e, k):
+            lo, hi = W_CUTS[e][k], W_CUTS[e][k + 1]
+            flat = w_raw[e][:, PASSES * PACK * lo : PASSES * PACK * hi]
+            return flat.rearrange("p (g t f) -> p g t f", g=PASSES, t=PACK), lo, hi
+
+        def load_w(e, k):
+            if k == 0:
+                w_raw[e] = work.tile([P, PASSES * PACK * F], BF16, name="w_raw", tag="w_raw")
+            piece, lo, hi = w_piece(e, k)
             for g in range(PASSES):
-                src = w_up[e, g * K_PASS : (g + 1) * K_PASS, cols].rearrange("(p t) f -> p t f", t=PACK)
-                nc.sync.dma_start(out=w_raw[e][:, g, :, cols], in_=src)
+                src = w_up[e, g * K_PASS : (g + 1) * K_PASS, lo:hi].rearrange("(p t) f -> p t f", t=PACK)
+                nc.sync.dma_start(out=piece[:, g, :, :], in_=src)
 
-        def load_x_codes(tokens):
-            src = x_words.rearrange("g p n t -> p g (n t)")
-            src = src[:, :, PACK * tokens.start : PACK * tokens.stop].bitcast(I32)
-            nc.sync.dma_start(out=x_codes[:, :, tokens].bitcast(I32), in_=src)
+        def load_x_codes(e):
+            src = x_words.rearrange("g p n t -> p g (n t)")[:, :, PACK * e * C : PACK * (e + 1) * C]
+            nc.sync.dma_start(out=x_codes[e][:].bitcast(I32), in_=src.bitcast(I32))
 
-        def load_x_scales(tokens):
+        def load_x_scales(plane, tokens):
             for q in range(4):
-                src = x_scales[:, 4 * q : 4 * q + 4, tokens].rearrange("g r n -> r g n").bitcast(I32)
-                nc.sync.dma_start(out=x_plane[32 * q : 32 * q + 4, :, tokens].bitcast(I32), in_=src)
+                src = x_scales[:, 4 * q : 4 * q + 4, tokens].rearrange("g r n -> r g n")
+                nc.sync.dma_start(out=plane[32 * q : 32 * q + 4, :, :].bitcast(I32), in_=src.bitcast(I32))
 
-        load_w(0, slice(0, 256))
-        load_x_scales(slice(0, C))
-        load_x_codes(slice(0, C))
-        load_w(0, slice(256, 512))
-        load_w(0, slice(512, 1024))
-        load_w(0, slice(1024, F))
-        load_x_scales(slice(C, E * C))
-        load_x_codes(slice(C, E * C))
-        load_w(1, slice(0, F))
-        load_w(2, slice(0, F))
+        load_w(0, 0)
+        load_x_scales(x_plane_first, slice(0, C))
+        load_x_codes(0)
+        load_w(0, 1)
+        load_w(0, 2)
+        load_w(1, 0)
+        load_x_scales(x_plane_rest, slice(C, E * C))
+        load_x_codes(1)
+        load_w(1, 1)
+        load_w(2, 0)
+        load_x_codes(2)
+        load_x_codes(3)
 
         w_grouped, w_codes, w_plane = {}, {}, {}
         acc, h, h_t, squares, y, y_bf16, words_t, y_grouped, y_codes = {}, {}, {}, {}, {}, {}, {}, {}, {}
 
-        def interleave_views(s, lo, hi):
+        def interleave(copy, s, g, lo, hi):
+            if s not in w_grouped:
+                w_grouped[s] = work.tile(
+                    [P, PASSES, CHUNK, PACK], BF16, name="w_grouped", tag="w_grouped", bufs=4, align_bytes=64
+                )
             e, first = divmod(s * CHUNK, F)
-            dst = w_grouped[s][:, :, lo:hi, :]
-            src = w_raw[e][:, :, :, first + lo : first + hi]
-            return dst, src
+            k = max(i for i, cut in enumerate(W_CUTS[e]) if cut <= first)
+            piece, start, end = w_piece(e, k)
+            copy(
+                out=w_grouped[s][:, g, lo:hi, :].rearrange("p (c i) t -> p c t i", i=4),
+                in_=piece[:, g, :, first - start + lo : first - start + hi].rearrange("p t (c i) -> p c t i", i=4),
+            )
+
+        def activation_copy(out, in_):
+            nc.scalar.activation(out=out, in_=in_, func=ACT.Copy)
 
         def interleave_scalar(s):
-            w_grouped[s] = work.tile([P, PASSES, CHUNK, PACK], BF16, name="w_grouped", tag="w_grouped", align_bytes=64)
-            dst, src = interleave_views(s, 0, scalar_columns(s))
-            if s == 0:
-                nc.scalar.activation(out=dst, in_=src.rearrange("p g t c -> p g c t"), func=ACT.Copy)
-            else:
-                nc.scalar.copy(
-                    out=dst.rearrange("p g (c i) t -> p g c t i", i=4),
-                    in_=src.rearrange("p g t (c i) -> p g c t i", i=4),
-                )
+            interleave(activation_copy if s == 0 else nc.scalar.copy, s, 1, CHUNK - scalar_columns(s), CHUNK)
 
-        def interleave_vector(s):
-            dst, src = interleave_views(s, scalar_columns(s), CHUNK)
-            nc.vector.tensor_copy(
-                out=dst.rearrange("p g (c i) t -> p g c t i", i=4),
-                in_=src.rearrange("p g t (c i) -> p g c t i", i=4),
-            )
+        def interleave_vector(s, g):
+            interleave(nc.vector.tensor_copy, s, g, 0, CHUNK - scalar_columns(s) if g == 1 else CHUNK)
 
         def quantize_w(s):
             w_codes[s] = work.tile([P, PASSES * CHUNK], U32, name="w_codes", tag="w_codes", bufs=4, align_bytes=64)
@@ -129,7 +133,6 @@ def tile_expert_up_squared_relu_g6_kernel(
 
         def multiply(s):
             e = s // STEPS_PER_EXPERT
-            tokens = slice(e * C, (e + 1) * C)
             for j in range(2):
                 acc[s, j] = psum.tile([P, C], F32, name="acc", tag="acc")
                 for g in range(PASSES):
@@ -138,21 +141,22 @@ def tile_expert_up_squared_relu_g6_kernel(
                         out=acc[s, j][:],
                         lhsT=w_codes[s][:, cols].bitcast(FP8X4),
                         lhsT_scale=w_plane[s][:, cols],
-                        rhs=x_codes[:, g, tokens].bitcast(FP8X4),
-                        rhs_scale=x_plane[:, g, tokens],
+                        rhs=x_codes[e][:, g, :].bitcast(FP8X4),
+                        rhs_scale=x_plane_first[:, g, :] if e == 0 else x_plane_rest[:, g, (e - 1) * C : e * C],
                         start=(g == 0),
                         stop=(g == PASSES - 1),
                     )
 
-        def bias_relu(s):
+        def bias_relu(s, j, on_vector):
             unit, half = divmod(s, 2)
-            if half == 0:
+            if unit not in h:
                 h[unit] = work.tile([P, 4, C], F32, name="h", tag="h", bufs=2)
-            for j in range(2):
-                col = 2 * s + j
-                nc.scalar.activation(
-                    out=h[unit][:, 2 * half + j, :], in_=acc[s, j][:], func=ACT.Relu, bias=columns[:, col : col + 1]
-                )
+            dst = h[unit][:, 2 * half + j, :]
+            bias = columns[:, 2 * s + j : 2 * s + j + 1]
+            if on_vector:
+                nc.vector.tensor_scalar(out=dst, in0=acc[s, j][:], scalar1=bias, scalar2=0.0, op0=ALU.add, op1=ALU.max)
+            else:
+                nc.scalar.activation(out=dst, in_=acc[s, j][:], func=ACT.Relu, bias=bias)
 
         def transpose_h(s):
             unit, half = divmod(s, 2)
@@ -161,7 +165,7 @@ def tile_expert_up_squared_relu_g6_kernel(
                 h_t[s, i] = psum.tile([P, K_PASS], F32, name="h_t", tag="h_t")
                 for j in range(4):
                     nc.tensor.transpose(
-                        h_t[s, i][:, j * P : (j + 1) * P], h[unit][:, j, m * P : (m + 1) * P], identity_f32[:]
+                        h_t[s, i][:, j * P : (j + 1) * P], h[unit][:, j, m * P : (m + 1) * P], identity[:]
                     )
 
         def square(s):
@@ -174,14 +178,22 @@ def tile_expert_up_squared_relu_g6_kernel(
             e, g = divmod(unit, GROUPS)
             return e, g, half
 
+        def y_columns(s):
+            e, g, half = place(s)
+            if e == E - 1:
+                return y[s][:]
+            return y[e, half][:, :, g * K_PASS : (g + 1) * K_PASS]
+
         def weigh(s):
             e, g, half = place(s)
-            if g == 0:
+            if e == E - 1:
+                y[s] = work.tile([P, 2, K_PASS], F32, name="y_last", tag="y", bufs=4)
+            elif g == 0:
                 y[e, half] = work.tile([P, 2, F], F32, name="y", tag="y", bufs=4)
             for i in range(2):
                 col = 48 + 4 * e + 2 * half + i
                 nc.vector.tensor_scalar(
-                    out=y[e, half][:, i, g * K_PASS : (g + 1) * K_PASS],
+                    out=y_columns(s)[:, i, :],
                     in0=squares[s][:, i, :],
                     scalar1=columns[:, col : col + 1],
                     scalar2=None,
@@ -192,65 +204,87 @@ def tile_expert_up_squared_relu_g6_kernel(
             e, g, half = place(s)
             dst = out_0[e, half * 2 * P : (half + 1) * 2 * P, :].rearrange("(i p) f -> p i f", p=P)
             if e == E - 1:
-                cols = slice(g * K_PASS, (g + 1) * K_PASS)
-                nc.sync.dma_start(out=dst[:, :, cols], in_=y[e, half][:, :, cols])
+                nc.sync.dma_start(out=dst[:, :, g * K_PASS : (g + 1) * K_PASS], in_=y[s][:])
             elif g == GROUPS - 1:
                 nc.sync.dma_start(out=dst, in_=y[e, half][:])
 
+        def parts(s):
+            return [(0, 1), (1, 2)] if s == STEPS - 1 else [(0, 2)]
+
         def round_y(s):
-            e, g, half = place(s)
-            y_bf16[s] = work.tile([P, 2 * K_PASS], BF16, name="y_bf16", tag="y_bf16")
-            nc.vector.tensor_copy(
-                out=y_bf16[s][:].rearrange("p (i u c b) -> p i u c b", i=2, u=2, b=2),
-                in_=y[e, half][:, :, g * K_PASS : (g + 1) * K_PASS].rearrange("p i (c u b) -> p i u c b", u=2, b=2),
-            )
+            y_bf16[s] = work.tile([P, 2, K_PASS], BF16, name="y_bf16", tag="y_bf16")
+            for lo, hi in parts(s):
+                nc.vector.tensor_copy(
+                    out=y_bf16[s][:, lo:hi, :].rearrange("p i (u c b) -> p i u c b", u=2, b=2),
+                    in_=y_columns(s)[:, lo:hi, :].rearrange("p i (c u b) -> p i u c b", u=2, b=2),
+                )
 
         def transpose_y(s):
-            words_t[s] = psum.tile([P, 4, P], F32, name="words_t", tag="words_t", bufs=2)
-            pairs = y_bf16[s][:].bitcast(F32)
-            for k in range(4):
-                nc.tensor.transpose(words_t[s][:, k, :], pairs[:, k * P : (k + 1) * P], identity_f32[:])
+            pairs = y_bf16[s][:].rearrange("p i f -> p (i f)").bitcast(F32)
+            for lo, hi in parts(s):
+                words_t[s, lo] = psum.tile([P, 2 * (hi - lo), P], F32, name="words_t", tag="words_t", bufs=2)
+                for k in range(2 * lo, 2 * hi):
+                    nc.tensor.transpose(words_t[s, lo][:, k - 2 * lo, :], pairs[:, k * P : (k + 1) * P], identity[:])
 
-        def group_y(s):
-            y_grouped[s] = work.tile([P, 2 * P * PACK], BF16, name="y_grouped", tag="y_grouped", align_bytes=64)
-            nc.scalar.copy(
-                out=y_grouped[s][:].bitcast(F32).rearrange("p (i n u) -> p i n u", i=2, u=2),
-                in_=words_t[s][:].rearrange("p (i u) n -> p i n u", u=2),
+        def group_y(s, lo, hi, copy):
+            if s not in y_grouped:
+                y_grouped[s] = work.tile([P, 2, P * PACK], BF16, name="y_grouped", tag="y_grouped", align_bytes=64)
+            copy(
+                out=y_grouped[s][:, lo:hi, :].bitcast(F32).rearrange("p i (n u) -> p i n u", u=2),
+                in_=words_t[s, lo][:].rearrange("p (i u) n -> p i n u", u=2),
             )
 
         def quantize_y(s):
             e, g, half = place(s)
             unit = s // 2
             if half == 0:
-                y_codes[unit] = work.tile([P, C], U32, name="y_codes", tag="y_codes", bufs=6, align_bytes=64)
-            first = e * C + half * 2 * P
-            nc.vector.quantize_mx(
-                out=y_codes[unit][:, half * 2 * P : (half + 1) * 2 * P].bitcast(FP8X4),
-                scales=y_plane[:, g, first : first + 2 * P],
-                in_=y_grouped[s][:],
-            )
+                y_codes[unit] = work.tile([P, C], U32, name="y_codes", tag="y_codes", bufs=5, align_bytes=64)
+            plane = y_plane_last[:, g, :] if e == E - 1 else y_plane_rest[:, g, e * C : (e + 1) * C]
+            for lo, hi in parts(s):
+                tokens = slice((2 * half + lo) * P, (2 * half + hi) * P)
+                nc.vector.quantize_mx(
+                    out=y_codes[unit][:, tokens].bitcast(FP8X4),
+                    scales=plane[:, tokens],
+                    in_=y_grouped[s][:, lo:hi, :].rearrange("p i n -> p (i n)"),
+                )
+
+        def store_scales(engine, plane, tokens):
+            for q in range(4):
+                dst = out_2[:, 4 * q : 4 * q + 4, tokens].rearrange("g r n -> r g n")
+                engine.dma_start(out=dst.bitcast(I32), in_=plane[32 * q : 32 * q + 4, :, :].bitcast(I32))
 
         def store_planes(s):
             e, g, half = place(s)
-            if half == 0:
-                return
             dst = out_1[g].rearrange("p n t -> p (n t)")[:, PACK * e * C : PACK * (e + 1) * C].bitcast(I32)
-            nc.sync.dma_start(out=dst, in_=y_codes[s // 2][:].bitcast(I32))
-            if e == E - 1:
-                for q in range(4):
-                    nc.sync.dma_start(
-                        out=out_2[g, 4 * q : 4 * q + 4, :].bitcast(I32),
-                        in_=y_plane[32 * q : 32 * q + 4, g, :].bitcast(I32),
-                    )
+            src = y_codes[s // 2][:].bitcast(I32)
+            if s >= STEPS - 2:
+                tokens = slice(half * 2 * P, (half + 1) * 2 * P)
+                nc.sync.dma_start(out=dst[:, tokens], in_=src[:, tokens])
+            elif half == 1:
+                nc.sync.dma_start(out=dst, in_=src)
+            if s == STEPS - STEPS_PER_EXPERT - 1:
+                store_scales(nc.sync, y_plane_rest, slice(0, (E - 1) * C))
+            if s == STEPS - 1:
+                store_scales(nc.scalar, y_plane_last, slice((E - 1) * C, E * C))
 
         def live(s):
             return 0 <= s < STEPS
 
-        for s in range(-3, STEPS + 5):
-            if s == -2:
-                rows_t = psum.tile([P, P], BF16, name="rows_t", tag="words_t", bufs=2)
-                nc.tensor.transpose(rows_t[:], rows[:], identity_bf16[:])
-                nc.scalar.copy(out=columns[:], in_=rows_t[:, 0:64])
+        interleave_vector(0, 0)
+        interleave_vector(1, 0)
+        nc.vector.tensor_copy(out=rows_f32[:], in_=rows[:])
+        interleave_scalar(0)
+        interleave_scalar(1)
+        interleave_vector(0, 1)
+        interleave_vector(1, 1)
+        rows_t = psum.tile([P, P], F32, name="rows_t", tag="words_t", bufs=2)
+        nc.tensor.transpose(rows_t[:], rows_f32[:], identity[:])
+        nc.scalar.copy(out=columns[:], in_=rows_t[:, 0:64])
+        quantize_w(0)
+        quantize_w(1)
+
+        for s in range(STEPS + 5):
+            draining = not live(s + 2)
             if live(s):
                 multiply(s)
             if live(s - 2):
@@ -258,25 +292,36 @@ def tile_expert_up_squared_relu_g6_kernel(
             if live(s - 4):
                 transpose_y(s - 4)
             if live(s):
-                bias_relu(s)
+                if not draining:
+                    bias_relu(s, 0, False)
+                bias_relu(s, 1, False)
+            if s == 0:
+                interleave_scalar(2)
             if live(s - 2):
                 square(s - 2)
             if live(s - 4):
-                group_y(s - 4)
+                group_y(s - 4, *parts(s - 4)[-1], nc.scalar.copy)
             if live(s + 3):
                 interleave_scalar(s + 3)
             if live(s + 2):
-                interleave_vector(s + 2)
+                interleave_vector(s + 2, 0)
+                interleave_vector(s + 2, 1)
             if live(s - 3):
                 weigh(s - 3)
+            if live(s) and draining:
+                bias_relu(s, 0, True)
             if live(s + 2):
                 quantize_w(s + 2)
+            if live(s - 5) and draining:
+                quantize_y(s - 5)
             if live(s - 3):
                 round_y(s - 3)
-            if live(s - 5):
+            if live(s - 5) and not draining:
                 quantize_y(s - 5)
+            if s - 4 == STEPS - 1:
+                group_y(s - 4, 0, 1, nc.vector.tensor_copy)
             if s + 2 == STEPS_PER_EXPERT - 1:
-                load_w(3, slice(0, F))
+                load_w(3, 0)
             if live(s - 3):
                 store_y(s - 3)
             if live(s - 5):

@@ -29,7 +29,7 @@ W_CUTS = [[0, 512, 1024, F], [0, 512, F], [0, F], [0, F]]
 
 
 def scalar_columns(s):
-    return 128 if s < 4 else 64
+    return 128 if 2 <= s < 6 else 64
 
 
 def tile_expert_up_squared_relu_g6_kernel(
@@ -131,21 +131,20 @@ def tile_expert_up_squared_relu_g6_kernel(
                 in_=w_grouped[s][:].rearrange("p g c t -> p (g c t)"),
             )
 
-        def multiply(s):
+        def multiply(s, j):
             e = s // STEPS_PER_EXPERT
-            for j in range(2):
-                acc[s, j] = psum.tile([P, C], F32, name="acc", tag="acc")
-                for g in range(PASSES):
-                    cols = slice(g * CHUNK + j * P, g * CHUNK + (j + 1) * P)
-                    nc.tensor.matmul_mx(
-                        out=acc[s, j][:],
-                        lhsT=w_codes[s][:, cols].bitcast(FP8X4),
-                        lhsT_scale=w_plane[s][:, cols],
-                        rhs=x_codes[e][:, g, :].bitcast(FP8X4),
-                        rhs_scale=x_plane_first[:, g, :] if e == 0 else x_plane_rest[:, g, (e - 1) * C : e * C],
-                        start=(g == 0),
-                        stop=(g == PASSES - 1),
-                    )
+            acc[s, j] = psum.tile([P, C], F32, name="acc", tag="acc")
+            for g in range(PASSES):
+                cols = slice(g * CHUNK + j * P, g * CHUNK + (j + 1) * P)
+                nc.tensor.matmul_mx(
+                    out=acc[s, j][:],
+                    lhsT=w_codes[s][:, cols].bitcast(FP8X4),
+                    lhsT_scale=w_plane[s][:, cols],
+                    rhs=x_codes[e][:, g, :].bitcast(FP8X4),
+                    rhs_scale=x_plane_first[:, g, :] if e == 0 else x_plane_rest[:, g, (e - 1) * C : e * C],
+                    start=(g == 0),
+                    stop=(g == PASSES - 1),
+                )
 
         def bias_relu(s, j, on_vector):
             unit, half = divmod(s, 2)
@@ -178,22 +177,13 @@ def tile_expert_up_squared_relu_g6_kernel(
             e, g = divmod(unit, GROUPS)
             return e, g, half
 
-        def y_columns(s):
-            e, g, half = place(s)
-            if e == E - 1:
-                return y[s][:]
-            return y[e, half][:, :, g * K_PASS : (g + 1) * K_PASS]
-
         def weigh(s):
             e, g, half = place(s)
-            if e == E - 1:
-                y[s] = work.tile([P, 2, K_PASS], F32, name="y_last", tag="y", bufs=4)
-            elif g == 0:
-                y[e, half] = work.tile([P, 2, F], F32, name="y", tag="y", bufs=4)
+            y[s] = work.tile([P, 2, K_PASS], F32, name="y", tag="y", bufs=12)
             for i in range(2):
                 col = 48 + 4 * e + 2 * half + i
                 nc.vector.tensor_scalar(
-                    out=y_columns(s)[:, i, :],
+                    out=y[s][:, i, :],
                     in0=squares[s][:, i, :],
                     scalar1=columns[:, col : col + 1],
                     scalar2=None,
@@ -202,11 +192,8 @@ def tile_expert_up_squared_relu_g6_kernel(
 
         def store_y(s):
             e, g, half = place(s)
-            dst = out_0[e, half * 2 * P : (half + 1) * 2 * P, :].rearrange("(i p) f -> p i f", p=P)
-            if e == E - 1:
-                nc.sync.dma_start(out=dst[:, :, g * K_PASS : (g + 1) * K_PASS], in_=y[s][:])
-            elif g == GROUPS - 1:
-                nc.sync.dma_start(out=dst, in_=y[e, half][:])
+            dst = out_0[e, half * 2 * P : (half + 1) * 2 * P, g * K_PASS : (g + 1) * K_PASS]
+            nc.sync.dma_start(out=dst.rearrange("(i p) f -> p i f", p=P), in_=y[s][:])
 
         def parts(s):
             return [(0, 1), (1, 2)] if s == STEPS - 1 else [(0, 2)]
@@ -216,7 +203,7 @@ def tile_expert_up_squared_relu_g6_kernel(
             for lo, hi in parts(s):
                 nc.vector.tensor_copy(
                     out=y_bf16[s][:, lo:hi, :].rearrange("p i (u c b) -> p i u c b", u=2, b=2),
-                    in_=y_columns(s)[:, lo:hi, :].rearrange("p i (c u b) -> p i u c b", u=2, b=2),
+                    in_=y[s][:, lo:hi, :].rearrange("p i (c u b) -> p i u c b", u=2, b=2),
                 )
 
         def transpose_y(s):
@@ -282,13 +269,16 @@ def tile_expert_up_squared_relu_g6_kernel(
         nc.scalar.copy(out=columns[:], in_=rows_t[:, 0:64])
         quantize_w(0)
         quantize_w(1)
+        multiply(0, 0)
 
         for s in range(STEPS + 5):
             draining = not live(s + 2)
             if live(s):
-                multiply(s)
+                multiply(s, 1)
             if live(s - 2):
                 transpose_h(s - 2)
+            if live(s + 1):
+                multiply(s + 1, 0)
             if live(s - 4):
                 transpose_y(s - 4)
             if live(s):

@@ -29,7 +29,9 @@ W_CUTS = [[0, 512, 1024, F], [0, 512, F], [0, F], [0, F]]
 
 
 def scalar_columns(s):
-    return 128 if 2 <= s < 6 else 64
+    if s < 4:
+        return CHUNK // 2
+    return CHUNK if s > STEPS_PER_EXPERT and s % 4 == 1 else 0
 
 
 def tile_expert_up_squared_relu_g6_kernel(
@@ -100,7 +102,7 @@ def tile_expert_up_squared_relu_g6_kernel(
         w_grouped, w_codes, w_plane = {}, {}, {}
         acc, h, h_t, squares, y, y_bf16, words_t, y_grouped, y_codes = {}, {}, {}, {}, {}, {}, {}, {}, {}
 
-        def interleave(copy, s, g, lo, hi):
+        def interleave(copy, s, passes, lo, hi):
             if s not in w_grouped:
                 w_grouped[s] = work.tile(
                     [P, PASSES, CHUNK, PACK], BF16, name="w_grouped", tag="w_grouped", bufs=4, align_bytes=64
@@ -109,18 +111,30 @@ def tile_expert_up_squared_relu_g6_kernel(
             k = max(i for i, cut in enumerate(W_CUTS[e]) if cut <= first)
             piece, start, end = w_piece(e, k)
             copy(
-                out=w_grouped[s][:, g, lo:hi, :].rearrange("p (c i) t -> p c t i", i=4),
-                in_=piece[:, g, :, first - start + lo : first - start + hi].rearrange("p t (c i) -> p c t i", i=4),
+                out=w_grouped[s][:, passes, lo:hi, :].rearrange("p g (c i) t -> p g c t i", i=4),
+                in_=piece[:, passes, :, first - start + lo : first - start + hi].rearrange(
+                    "p g t (c i) -> p g c t i", i=4
+                ),
             )
 
         def activation_copy(out, in_):
-            nc.scalar.activation(out=out, in_=in_, func=ACT.Copy)
+            nc.scalar.activation(out=out[:, 0, :, :, :], in_=in_[:, 0, :, :, :], func=ACT.Copy)
 
         def interleave_scalar(s):
-            interleave(activation_copy if s == 0 else nc.scalar.copy, s, 1, CHUNK - scalar_columns(s), CHUNK)
+            if scalar_columns(s):
+                copy = activation_copy if s == 0 else nc.scalar.copy
+                interleave(copy, s, slice(1, 2), CHUNK - scalar_columns(s), CHUNK)
 
         def interleave_vector(s, g):
-            interleave(nc.vector.tensor_copy, s, g, 0, CHUNK - scalar_columns(s) if g == 1 else CHUNK)
+            interleave(nc.vector.tensor_copy, s, slice(g, g + 1), 0, CHUNK - scalar_columns(s) if g == 1 else CHUNK)
+
+        def interleave_rest(s):
+            if scalar_columns(s) == 0:
+                interleave(nc.vector.tensor_copy, s, slice(0, PASSES), 0, CHUNK)
+            else:
+                interleave_vector(s, 0)
+                if scalar_columns(s) < CHUNK:
+                    interleave_vector(s, 1)
 
         def quantize_w(s):
             w_codes[s] = work.tile([P, PASSES * CHUNK], U32, name="w_codes", tag="w_codes", bufs=4, align_bytes=64)
@@ -213,11 +227,12 @@ def tile_expert_up_squared_relu_g6_kernel(
                 for k in range(2 * lo, 2 * hi):
                     nc.tensor.transpose(words_t[s, lo][:, k - 2 * lo, :], pairs[:, k * P : (k + 1) * P], identity[:])
 
-        def group_y(s, lo, hi, copy):
-            if s not in y_grouped:
-                y_grouped[s] = work.tile([P, 2, P * PACK], BF16, name="y_grouped", tag="y_grouped", align_bytes=64)
-            copy(
-                out=y_grouped[s][:, lo:hi, :].bitcast(F32).rearrange("p i (n u) -> p i n u", u=2),
+        def group_y(s, lo, hi):
+            unit, half = divmod(s, 2)
+            if unit not in y_grouped:
+                y_grouped[unit] = work.tile([P, 4, P * PACK], BF16, name="y_grouped", tag="y_grouped", align_bytes=64)
+            nc.scalar.copy(
+                out=y_grouped[unit][:, 2 * half + lo : 2 * half + hi, :].bitcast(F32).rearrange("p i (n u) -> p i n u", u=2),
                 in_=words_t[s, lo][:].rearrange("p (i u) n -> p i n u", u=2),
             )
 
@@ -227,12 +242,16 @@ def tile_expert_up_squared_relu_g6_kernel(
             if half == 0:
                 y_codes[unit] = work.tile([P, C], U32, name="y_codes", tag="y_codes", bufs=5, align_bytes=64)
             plane = y_plane_last[:, g, :] if e == E - 1 else y_plane_rest[:, g, e * C : (e + 1) * C]
-            for lo, hi in parts(s):
-                tokens = slice((2 * half + lo) * P, (2 * half + hi) * P)
+            if e == E - 1:
+                spans = [(2 * half + lo, 2 * half + hi) for lo, hi in parts(s)]
+            else:
+                spans = [(0, 4)] * half
+            for lo, hi in spans:
+                tokens = slice(lo * P, hi * P)
                 nc.vector.quantize_mx(
                     out=y_codes[unit][:, tokens].bitcast(FP8X4),
                     scales=plane[:, tokens],
-                    in_=y_grouped[s][:, lo:hi, :].rearrange("p i n -> p (i n)"),
+                    in_=y_grouped[unit][:, lo:hi, :].rearrange("p i n -> p (i n)"),
                 )
 
         def store_scales(engine, plane, tokens):
@@ -257,13 +276,17 @@ def tile_expert_up_squared_relu_g6_kernel(
         def live(s):
             return 0 <= s < STEPS
 
-        interleave_vector(0, 0)
-        interleave_vector(1, 0)
-        nc.vector.tensor_copy(out=rows_f32[:], in_=rows[:])
-        interleave_scalar(0)
-        interleave_scalar(1)
-        interleave_vector(0, 1)
-        interleave_vector(1, 1)
+        def prepare_pair(s):
+            interleave_vector(s, 0)
+            interleave_vector(s + 1, 0)
+            if s == 0:
+                nc.vector.tensor_copy(out=rows_f32[:], in_=rows[:])
+            interleave_scalar(s)
+            interleave_scalar(s + 1)
+            interleave_vector(s, 1)
+            interleave_vector(s + 1, 1)
+
+        prepare_pair(0)
         rows_t = psum.tile([P, P], F32, name="rows_t", tag="words_t", bufs=2)
         nc.tensor.transpose(rows_t[:], rows_f32[:], identity[:])
         nc.scalar.copy(out=columns[:], in_=rows_t[:, 0:64])
@@ -282,25 +305,28 @@ def tile_expert_up_squared_relu_g6_kernel(
             if live(s - 4):
                 transpose_y(s - 4)
             if live(s):
-                if not draining:
+                if s < STEPS - 1:
                     bias_relu(s, 0, False)
                 bias_relu(s, 1, False)
-            if s == 0:
-                interleave_scalar(2)
             if live(s - 2):
                 square(s - 2)
             if live(s - 4):
-                group_y(s - 4, *parts(s - 4)[-1], nc.scalar.copy)
-            if live(s + 3):
+                for lo, hi in parts(s - 4):
+                    group_y(s - 4, lo, hi)
+            if s < 2:
+                prepare_pair(2 * s + 2)
+                quantize_w(2 * s + 2)
+                quantize_w(2 * s + 3)
+            ahead = STEPS_PER_EXPERT <= s + 2 < STEPS
+            if STEPS_PER_EXPERT <= s + 3 < STEPS:
                 interleave_scalar(s + 3)
-            if live(s + 2):
-                interleave_vector(s + 2, 0)
-                interleave_vector(s + 2, 1)
+            if ahead:
+                interleave_rest(s + 2)
             if live(s - 3):
                 weigh(s - 3)
-            if live(s) and draining:
+            if s == STEPS - 1:
                 bias_relu(s, 0, True)
-            if live(s + 2):
+            if ahead:
                 quantize_w(s + 2)
             if live(s - 5) and draining:
                 quantize_y(s - 5)
@@ -308,9 +334,7 @@ def tile_expert_up_squared_relu_g6_kernel(
                 round_y(s - 3)
             if live(s - 5) and not draining:
                 quantize_y(s - 5)
-            if s - 4 == STEPS - 1:
-                group_y(s - 4, 0, 1, nc.vector.tensor_copy)
-            if s + 2 == STEPS_PER_EXPERT - 1:
+            if s == 1:
                 load_w(3, 0)
             if live(s - 3):
                 store_y(s - 3)

from contextlib import ExitStack

import concourse.mybir as mybir
from concourse.masks import make_identity

E, C, D, F = 4, 512, 1024, 1536
FLOPS = 2 * E * C * D * F

F32 = mybir.dt.float32
BF16 = mybir.dt.bfloat16
I32 = mybir.dt.int32
U32 = mybir.dt.uint32
U8 = mybir.dt.uint8
FP8X4 = mybir.dt.float8_e4m3fn_x4
ACT = mybir.ActivationFunctionType
ALU = mybir.AluOpType

P = 128
PACK = 4
K_PASS = P * PACK
PASSES = D // K_PASS
GROUPS = F // K_PASS
CHUNK = 256
STEPS_PER_EXPERT = F // CHUNK
STEPS = E * STEPS_PER_EXPERT


W_CUTS = [[0, 512, 1024, F], [0, 512, F], [0, F], [0, F]]


def scalar_columns(s):
    if s < 4:
        return CHUNK // 2
    return CHUNK if s > STEPS_PER_EXPERT and s % 4 == 1 else 0


def tile_expert_up_squared_relu_g6_kernel(
    tc, x_words, x_scales, w_up, b_up, router_weight, out_0, out_1, out_2
):
    nc = tc.nc

    with ExitStack() as ctx:
        keep = ctx.enter_context(tc.tile_pool(name="keep", bufs=1))
        work = ctx.enter_context(tc.tile_pool(name="work", bufs=3))
        psum = ctx.enter_context(tc.psum_pool(name="psum", bufs=3))
        ctx.enter_context(tc.manual_schedule())

        x_codes = [keep.tile([P, PASSES, C], U32, name="x_codes%d" % e, align_bytes=64) for e in range(E)]
        x_plane_first = keep.tile([P, PASSES, C], U8, align_bytes=64)
        x_plane_rest = keep.tile([P, PASSES, (E - 1) * C], U8, align_bytes=64)
        y_plane_rest = keep.tile([P, GROUPS, (E - 1) * C], U8, align_bytes=64)
        y_plane_last = keep.tile([P, GROUPS, C], U8, align_bytes=64)
        rows = keep.tile([P, P], BF16)
        rows_f32 = keep.tile([P, P], F32)
        columns = keep.tile([P, 64], F32)
        identity = keep.tile([P, P], F32)

        nc.vector.memset(rows[:], 0.0)
        nc.vector.memset(x_plane_first[:].rearrange("p g n -> p (g n)").bitcast(I32), 0)
        nc.vector.memset(x_plane_rest[:].rearrange("p g n -> p (g n)").bitcast(I32), 0)
        nc.scalar.dma_start(out=rows[0:48, :], in_=b_up.rearrange("e (j p) -> (e j) p", p=P))
        nc.scalar.dma_start(out=rows[48:64, :], in_=router_weight.rearrange("e (m p) -> (e m) p", p=P))
        make_identity(nc, identity[:])

        w_raw = {}

        def w_piece(e, k):
            lo, hi = W_CUTS[e][k], W_CUTS[e][k + 1]
            flat = w_raw[e][:, PASSES * PACK * lo : PASSES * PACK * hi]
            return flat.rearrange("p (g t f) -> p g t f", g=PASSES, t=PACK), lo, hi

        def load_w(e, k):
            if k == 0:
                w_raw[e] = work.tile([P, PASSES * PACK * F], BF16, name="w_raw", tag="w_raw")
            piece, lo, hi = w_piece(e, k)
            for g in range(PASSES):
                src = w_up[e, g * K_PASS : (g + 1) * K_PASS, lo:hi].rearrange("(p t) f -> p t f", t=PACK)
                nc.sync.dma_start(out=piece[:, g, :, :], in_=src)

        def load_x_codes(e):
            src = x_words.rearrange("g p n t -> p g (n t)")[:, :, PACK * e * C : PACK * (e + 1) * C]
            nc.sync.dma_start(out=x_codes[e][:].bitcast(I32), in_=src.bitcast(I32))

        def load_x_scales(plane, tokens):
            for q in range(4):
                src = x_scales[:, 4 * q : 4 * q + 4, tokens].rearrange("g r n -> r g n")
                nc.sync.dma_start(out=plane[32 * q : 32 * q + 4, :, :].bitcast(I32), in_=src.bitcast(I32))

        load_w(0, 0)
        load_x_scales(x_plane_first, slice(0, C))
        load_x_codes(0)
        load_w(0, 1)
        load_w(0, 2)
        load_w(1, 0)
        load_x_scales(x_plane_rest, slice(C, E * C))
        load_x_codes(1)
        load_w(1, 1)
        load_w(2, 0)
        load_x_codes(2)
        load_x_codes(3)

        w_grouped, w_codes, w_plane = {}, {}, {}
        acc, h, h_t, squares, y, y_bf16, words_t, y_grouped, y_codes = {}, {}, {}, {}, {}, {}, {}, {}, {}

        def interleave(copy, s, passes, lo, hi):
            if s not in w_grouped:
                w_grouped[s] = work.tile(
                    [P, PASSES, CHUNK, PACK], BF16, name="w_grouped", tag="w_grouped", bufs=4, align_bytes=64
                )
            e, first = divmod(s * CHUNK, F)
            k = max(i for i, cut in enumerate(W_CUTS[e]) if cut <= first)
            piece, start, end = w_piece(e, k)
            copy(
                out=w_grouped[s][:, passes, lo:hi, :].rearrange("p g (c i) t -> p g c t i", i=4),
                in_=piece[:, passes, :, first - start + lo : first - start + hi].rearrange(
                    "p g t (c i) -> p g c t i", i=4
                ),
            )

        def activation_copy(out, in_):
            nc.scalar.activation(out=out[:, 0, :, :, :], in_=in_[:, 0, :, :, :], func=ACT.Copy)

        def interleave_scalar(s):
            if scalar_columns(s):
                copy = activation_copy if s == 0 else nc.scalar.copy
                interleave(copy, s, slice(1, 2), CHUNK - scalar_columns(s), CHUNK)

        def interleave_vector(s, g):
            interleave(nc.vector.tensor_copy, s, slice(g, g + 1), 0, CHUNK - scalar_columns(s) if g == 1 else CHUNK)

        def interleave_rest(s):
            if scalar_columns(s) == 0:
                interleave(nc.vector.tensor_copy, s, slice(0, PASSES), 0, CHUNK)
            else:
                interleave_vector(s, 0)
                if scalar_columns(s) < CHUNK:
                    interleave_vector(s, 1)

        def quantize_w(s):
            w_codes[s] = work.tile([P, PASSES * CHUNK], U32, name="w_codes", tag="w_codes", bufs=4, align_bytes=64)
            w_plane[s] = work.tile([P, PASSES * CHUNK], U8, name="w_plane", tag="w_plane", bufs=4, align_bytes=64)
            nc.vector.quantize_mx(
                out=w_codes[s][:].bitcast(FP8X4),
                scales=w_plane[s][:],
                in_=w_grouped[s][:].rearrange("p g c t -> p (g c t)"),
            )

        def multiply(s, j):
            e = s // STEPS_PER_EXPERT
            acc[s, j] = psum.tile([P, C], F32, name="acc", tag="acc")
            for g in range(PASSES):
                cols = slice(g * CHUNK + j * P, g * CHUNK + (j + 1) * P)
                nc.tensor.matmul_mx(
                    out=acc[s, j][:],
                    lhsT=w_codes[s][:, cols].bitcast(FP8X4),
                    lhsT_scale=w_plane[s][:, cols],
                    rhs=x_codes[e][:, g, :].bitcast(FP8X4),
                    rhs_scale=x_plane_first[:, g, :] if e == 0 else x_plane_rest[:, g, (e - 1) * C : e * C],
                    start=(g == 0),
                    stop=(g == PASSES - 1),
                )

        def bias_relu(s, j, on_vector):
            unit, half = divmod(s, 2)
            if unit not in h:
                h[unit] = work.tile([P, 4, C], F32, name="h", tag="h", bufs=2)
            dst = h[unit][:, 2 * half + j, :]
            bias = columns[:, 2 * s + j : 2 * s + j + 1]
            if on_vector:
                nc.vector.tensor_scalar(out=dst, in0=acc[s, j][:], scalar1=bias, scalar2=0.0, op0=ALU.add, op1=ALU.max)
            else:
                nc.scalar.activation(out=dst, in_=acc[s, j][:], func=ACT.Relu, bias=bias)

        def transpose_h(s):
            unit, half = divmod(s, 2)
            for i in range(2):
                m = 2 * half + i
                h_t[s, i] = psum.tile([P, K_PASS], F32, name="h_t", tag="h_t")
                for j in range(4):
                    nc.tensor.transpose(
                        h_t[s, i][:, j * P : (j + 1) * P], h[unit][:, j, m * P : (m + 1) * P], identity[:]
                    )

        def square(s):
            squares[s] = work.tile([P, 2, K_PASS], F32, name="squares", tag="squares")
            for i in range(2):
                nc.scalar.activation(out=squares[s][:, i, :], in_=h_t[s, i][:], func=ACT.Square)

        def place(s):
            unit, half = divmod(s, 2)
            e, g = divmod(unit, GROUPS)
            return e, g, half

        def weigh(s):
            e, g, half = place(s)
            y[s] = work.tile([P, 2, K_PASS], F32, name="y", tag="y", bufs=12)
            for i in range(2):
                col = 48 + 4 * e + 2 * half + i
                nc.vector.tensor_scalar(
                    out=y[s][:, i, :],
                    in0=squares[s][:, i, :],
                    scalar1=columns[:, col : col + 1],
                    scalar2=None,
                    op0=ALU.mult,
                )

        def store_y(s):
            e, g, half = place(s)
            dst = out_0[e, half * 2 * P : (half + 1) * 2 * P, g * K_PASS : (g + 1) * K_PASS]
            nc.sync.dma_start(out=dst.rearrange("(i p) f -> p i f", p=P), in_=y[s][:])

        def parts(s):
            return [(0, 1), (1, 2)] if s == STEPS - 1 else [(0, 2)]

        def round_y(s):
            y_bf16[s] = work.tile([P, 2, K_PASS], BF16, name="y_bf16", tag="y_bf16")
            for lo, hi in parts(s):
                nc.vector.tensor_copy(
                    out=y_bf16[s][:, lo:hi, :].rearrange("p i (u c b) -> p i u c b", u=2, b=2),
                    in_=y[s][:, lo:hi, :].rearrange("p i (c u b) -> p i u c b", u=2, b=2),
                )

        def transpose_y(s):
            pairs = y_bf16[s][:].rearrange("p i f -> p (i f)").bitcast(F32)
            for lo, hi in parts(s):
                words_t[s, lo] = psum.tile([P, 2 * (hi - lo), P], F32, name="words_t", tag="words_t", bufs=2)
                for k in range(2 * lo, 2 * hi):
                    nc.tensor.transpose(words_t[s, lo][:, k - 2 * lo, :], pairs[:, k * P : (k + 1) * P], identity[:])

        def group_y(s, lo, hi):
            unit, half = divmod(s, 2)
            if unit not in y_grouped:
                y_grouped[unit] = work.tile([P, 4, P * PACK], BF16, name="y_grouped", tag="y_grouped", align_bytes=64)
            nc.scalar.copy(
                out=y_grouped[unit][:, 2 * half + lo : 2 * half + hi, :].bitcast(F32).rearrange("p i (n u) -> p i n u", u=2),
                in_=words_t[s, lo][:].rearrange("p (i u) n -> p i n u", u=2),
            )

        def quantize_y(s):
            e, g, half = place(s)
            unit = s // 2
            if half == 0:
                y_codes[unit] = work.tile([P, C], U32, name="y_codes", tag="y_codes", bufs=5, align_bytes=64)
            plane = y_plane_last[:, g, :] if e == E - 1 else y_plane_rest[:, g, e * C : (e + 1) * C]
            if e == E - 1:
                spans = [(2 * half + lo, 2 * half + hi) for lo, hi in parts(s)]
            else:
                spans = [(0, 4)] * half
            for lo, hi in spans:
                tokens = slice(lo * P, hi * P)
                nc.vector.quantize_mx(
                    out=y_codes[unit][:, tokens].bitcast(FP8X4),
                    scales=plane[:, tokens],
                    in_=y_grouped[unit][:, lo:hi, :].rearrange("p i n -> p (i n)"),
                )

        def store_scales(engine, plane, tokens):
            for q in range(4):
                dst = out_2[:, 4 * q : 4 * q + 4, tokens].rearrange("g r n -> r g n")
                engine.dma_start(out=dst.bitcast(I32), in_=plane[32 * q : 32 * q + 4, :, :].bitcast(I32))

        def store_planes(s):
            e, g, half = place(s)
            dst = out_1[g].rearrange("p n t -> p (n t)")[:, PACK * e * C : PACK * (e + 1) * C].bitcast(I32)
            src = y_codes[s // 2][:].bitcast(I32)
            if s >= STEPS - 2:
                tokens = slice(half * 2 * P, (half + 1) * 2 * P)
                nc.sync.dma_start(out=dst[:, tokens], in_=src[:, tokens])
            elif half == 1:
                nc.sync.dma_start(out=dst, in_=src)
            if s == STEPS - STEPS_PER_EXPERT - 1:
                store_scales(nc.sync, y_plane_rest, slice(0, (E - 1) * C))
            if s == STEPS - 1:
                store_scales(nc.scalar, y_plane_last, slice((E - 1) * C, E * C))

        def live(s):
            return 0 <= s < STEPS

        def prepare_pair(s):
            interleave_vector(s, 0)
            interleave_vector(s + 1, 0)
            if s == 0:
                nc.vector.tensor_copy(out=rows_f32[:], in_=rows[:])
            interleave_scalar(s)
            interleave_scalar(s + 1)
            interleave_vector(s, 1)
            interleave_vector(s + 1, 1)

        prepare_pair(0)
        rows_t = psum.tile([P, P], F32, name="rows_t", tag="words_t", bufs=2)
        nc.tensor.transpose(rows_t[:], rows_f32[:], identity[:])
        nc.scalar.copy(out=columns[:], in_=rows_t[:, 0:64])
        quantize_w(0)
        quantize_w(1)
        multiply(0, 0)

        for s in range(STEPS + 5):
            draining = not live(s + 2)
            if live(s):
                multiply(s, 1)
            if live(s - 2):
                transpose_h(s - 2)
            if live(s + 1):
                multiply(s + 1, 0)
            if live(s - 4):
                transpose_y(s - 4)
            if live(s):
                if s < STEPS - 1:
                    bias_relu(s, 0, False)
                bias_relu(s, 1, False)
            if live(s - 2):
                square(s - 2)
            if live(s - 4):
                for lo, hi in parts(s - 4):
                    group_y(s - 4, lo, hi)
            if s < 2:
                prepare_pair(2 * s + 2)
                quantize_w(2 * s + 2)
                quantize_w(2 * s + 3)
            ahead = STEPS_PER_EXPERT <= s + 2 < STEPS
            if STEPS_PER_EXPERT <= s + 3 < STEPS:
                interleave_scalar(s + 3)
            if ahead:
                interleave_rest(s + 2)
            if live(s - 3):
                weigh(s - 3)
            if s == STEPS - 1:
                bias_relu(s, 0, True)
            if ahead:
                quantize_w(s + 2)
            if live(s - 5) and draining:
                quantize_y(s - 5)
            if live(s - 3):
                round_y(s - 3)
            if live(s - 5) and not draining:
                quantize_y(s - 5)
            if s == 1:
                load_w(3, 0)
            if live(s - 3):
                store_y(s - 3)
            if live(s - 5):
                store_planes(s - 5)
